import numpy as np
import ml_dtypes


def mxq(x, axis, fmt="e4m3"):
    dtype, down = {"e4m3": (ml_dtypes.float8_e4m3fn, 7), "e5m2": (ml_dtypes.float8_e5m2, 14)}[fmt]
    v = np.moveaxis(np.asarray(x, np.float32).astype(ml_dtypes.bfloat16).astype(np.float64), axis, -1)
    blocks = v.reshape(v.shape[:-1] + (-1, 32))
    amax = np.abs(blocks).max(-1, keepdims=True)
    byte = np.maximum(np.where(amax > 0, np.frexp(amax)[1] - 1 + 127, 0) - down, 1)
    scale = np.exp2(byte - 127.0)
    codes = (blocks / scale).astype(np.float32).astype(dtype).astype(np.float64)
    return np.moveaxis((codes * scale).reshape(v.shape), -1, axis)


WIDE = False


def mx_kscale(k):
    if not WIDE:
        return np.ones(k)
    levels = np.array([10, -10, 5, -5, 0])
    if k % 512:
        return np.exp2(np.random.permutation(np.resize(levels, k // 32))).repeat(32)
    a = np.empty((k // 512, 16))
    for p in range(k // 512):
        a[p, :8] = np.random.permutation(np.resize(levels, 8))
        for g in range(8):
            far = levels[np.abs(levels - a[p, g]) >= 10]
            a[p, g + 8] = far[np.random.randint(len(far))]
    return np.exp2(a.ravel()).repeat(32)


def f64(x):
    return np.asarray(x).astype(np.float64)


def striped(idx):
    return np.tile(np.asarray(idx).reshape(-1, 16).T, (8, 1)).astype(np.uint16)


def unstriped(offs):
    return offs[:16].T.reshape(-1).astype(np.int64)


E2M1 = np.array([0.0, 0.5, 1.0, 1.5, 2.0, 3.0, 4.0, 6.0, -0.0, -0.5, -1.0, -1.5, -2.0, -3.0, -4.0, -6.0])


def pack_weight(w, fmt):
    k, n = w.shape
    w = f64(np.asarray(w, np.float32).astype(ml_dtypes.bfloat16)).reshape(k // 32, 32, n)
    amax = np.abs(w).max(1)
    if fmt == "e4m3":
        byte = np.frexp(amax)[1] - 1 + 127 - 7
    else:
        mant, ex = np.frexp(amax / 6.0)
        byte = np.where(mant > 0.5, ex, ex - 1) + 127
    byte = np.clip(np.where(amax > 0, byte, 1), 1, 254)
    scaled = (w * np.exp2(127.0 - byte)[:, None, :]).reshape(k, n).astype(np.float32)
    by_word = np.ascontiguousarray(scaled.reshape(k // 512, 128, 4, n).transpose(0, 1, 3, 2))
    if fmt == "e4m3":
        words = by_word.astype(ml_dtypes.float8_e4m3fn).view(np.uint8)
    else:
        c = by_word.astype(ml_dtypes.float4_e2m1fn).view(np.uint8) & 0xF
        words = (c[..., 0::2] | (c[..., 1::2] << 4)).reshape(k // 512, 128, 2 * n)
    return np.ascontiguousarray(words), np.ascontiguousarray(byte.astype(np.uint8).reshape(k // 512, 16, n))


def unpack_weight(words, scales, fmt):
    g, _, n = scales.shape
    words = np.ascontiguousarray(words).reshape(g, 128, n, -1)
    if fmt == "e4m3":
        vals = words.view(ml_dtypes.float8_e4m3fn).astype(np.float64)
    else:
        nib = np.empty((g, 128, n, 4), np.uint8)
        nib[..., 0::2] = words & 0xF
        nib[..., 1::2] = words >> 4
        vals = E2M1[nib]
    vals = vals * np.repeat(np.exp2(scales.astype(np.float64) - 127.0), 8, axis=1)[..., None]
    return vals.transpose(0, 1, 3, 2).reshape(g * 512, n)


K, T, I, F, M, G = 512, 2048, 1024, 512, 128, 64


def setup_inputs():
    n = np.random.standard_normal
    idx = np.random.permutation(T)[:I]
    idx2 = np.repeat(np.random.permutation(T)[:G], I // G)
    fk = mx_kscale(K)
    ff = mx_kscale(F)
    xp = pack_weight(n((K, T)) / fk[:, None], "e4m3")
    return {
        "x_words": xp[0],
        "x_scales": xp[1],
        "wl": (n((K, F)) * 1 / np.sqrt(K) * fk[:, None] * ff).astype(np.float32),
        "wr": (n((K, F)) * 1 / np.sqrt(K) * fk[:, None] * ff).astype(np.float32),
        "att": (n((F, M)) * 1 / np.sqrt(F) / ff[:, None]).astype(np.float32),
        "offs": striped(idx),
        "offs2": striped(idx2),
    }


def reference(x_words, x_scales, wl, wr, att, offs, offs2):
    idx = unstriped(offs)
    idx2 = unstriped(offs2)
    xu = unpack_weight(x_words, x_scales, "e4m3")
    wlq = mxq(f64(wl), 0, "e4m3")
    xidxg = xu[:, idx]
    wrq = mxq(f64(wr), 0, "e4m3")
    xidx2g = xu[:, idx2]
    z = wlq.T @ xidxg + wrq.T @ xidx2g
    lz = np.maximum(z, 0.2 * z)
    attq = mxq(f64(att), 0, "e4m3")
    lzq = mxq(lz, 0, "e4m3")
    b = attq.T @ lzq
    p = np.exp(b)
    s = p.reshape(M, G, I // G).sum(axis=2)
    sr = np.repeat(s, I // G, axis=1)
    y = p / sr * 16.0
    return y

@@ -1,0 +1,199 @@
+from contextlib import ExitStack
+
+import concourse.mybir as mybir
+
+K, T, I, F, M, G = 512, 2048, 1024, 512, 128, 64
+FLOPS = 2 * K * F * I * 2 + 2 * F * M * I
+
+F32 = mybir.dt.float32
+BF16 = mybir.dt.bfloat16
+I32 = mybir.dt.int32
+U32 = mybir.dt.uint32
+U16 = mybir.dt.uint16
+U8 = mybir.dt.uint8
+FP8X4 = mybir.dt.float8_e4m3fn_x4
+ALU = mybir.AluOpType
+ACT = mybir.ActivationFunctionType
+AXIS_X = mybir.AxisListType.X
+
+P = 128
+PACK = 4
+DEG = I // G
+SLOPE = 0.2
+BANK_EDGES = 128
+GATHER_EDGES = 256
+HALVES = 2
+CHUNKS = [256,256,256,256]
+TWO_READ_BANKS = 8
+
+
+def tile_attend_gatv2_kernel(tc, x_words, x_scales, wl, wr, att, offs, offs2, out):
+    nc = tc.nc
+    with ExitStack() as ctx:
+        keep = ctx.enter_context(tc.tile_pool(name="keep", bufs=1))
+        work = ctx.enter_context(tc.tile_pool(name="work", bufs=4))
+        zpsum = ctx.enter_context(tc.psum_pool(name="zpsum", bufs=6))
+        bpsum = ctx.enter_context(tc.psum_pool(name="bpsum", bufs=2))
+
+        lists = []
+        for name, src in (("src_list", offs), ("dst_list", offs2)):
+            tile = keep.tile([P, I // 16], U16, name=name)
+            nc.sync.dma_start(tile[:], src)
+            lists.append(tile)
+
+        x_bytes = keep.tile([P, T], U8, name="x_bytes", align_bytes=64)
+        nc.vector.memset(x_bytes[:].bitcast(I32), 0)
+        for q in range(4):
+            nc.sync.dma_start(x_bytes[32 * q : 32 * q + 4, :].bitcast(I32), x_scales[0, 4 * q : 4 * q + 4, :].bitcast(I32))
+
+        warm = keep.tile([P, 1], F32, name="warm")
+        warm_out = keep.tile([P, 1], F32, name="warm_out")
+        nc.gpsimd.memset(warm[:], 0.0)
+        nc.scalar.activation(out=warm_out[:], in_=warm[:], func=ACT.Exp)
+
+        half = F // HALVES
+        w_raw = []
+        for name, w in (("wl", wl), ("wr", wr)):
+            rows = w.rearrange("(p j) f -> p j f", j=PACK)
+            for c in range(HALVES):
+                raw = keep.tile([P, PACK, half], F32, name="%s_raw%d" % (name, c))
+                nc.sync.dma_start(raw[:], rows[:, :, c * half : (c + 1) * half])
+                w_raw.append(raw)
+
+        x_tile = keep.tile([P, T], U32, name="x_tile", align_bytes=64)
+        nc.sync.dma_start(x_tile[:].bitcast(I32), x_words[0].rearrange("p n t -> p (n t)").bitcast(I32))
+
+        att_raw = keep.tile([P, PACK, M], F32, name="att_raw")
+        att_rows = att.rearrange("(u t r) m -> r u t m", t=PACK, r=4)
+        for r in range(4):
+            nc.sync.dma_start(att_raw[r:P:4, :, :], att_rows[r])
+
+        edge_bytes = []
+        for s in range(2):
+            picked = keep.tile([P, I], U8, name="edge_bytes%d" % s, align_bytes=64)
+            nc.vector.tensor_copy(out=picked[:], in_=x_bytes[:].indirect(lists[s][:]))
+            edge_bytes.append(picked)
+
+        w_codes, w_bytes = [], []
+        for s in range(2):
+            grouped = keep.tile([P, PACK, HALVES, half // 16, 4, PACK], BF16, name="w_grouped%d" % s, align_bytes=64)
+            for c in range(HALVES):
+                nc.scalar.copy(
+                    out=grouped[:, :, c, :, :, :].rearrange("p t u r j -> p t u j r"),
+                    in_=w_raw[HALVES * s + c][:].rearrange("p j (u t r) -> p t u j r", t=PACK, r=4),
+                )
+            codes = keep.tile([P, F], U32, name="w_codes%d" % s, align_bytes=64)
+            scales = keep.tile([P, F], U8, name="w_bytes%d" % s, align_bytes=64)
+            nc.vector.quantize_mx(
+                out=codes[:].bitcast(FP8X4), scales=scales[:], in_=grouped[:].rearrange("p t c u r j -> p (t c u r j)")
+            )
+            w_codes.append(codes)
+            w_bytes.append(scales)
+
+        edge_words = [[], []]
+        for c in range(I // GATHER_EDGES):
+            cols = slice(c * GATHER_EDGES // 16, (c + 1) * GATHER_EDGES // 16)
+            for s in range(2):
+                picked = keep.tile([P, GATHER_EDGES], U32, name="edge_words%d_%d" % (s, c), align_bytes=64)
+                nc.vector.tensor_copy(out=picked[:], in_=x_tile[:].indirect(lists[s][:, cols]))
+                edge_words[s].append(picked)
+
+        att_grouped = keep.tile([P, M, PACK], BF16, name="att_grouped", align_bytes=64)
+        nc.scalar.copy(
+            out=att_grouped[:].rearrange("p (c i) t -> p c t i", i=4),
+            in_=att_raw[:].rearrange("p t (c i) -> p c t i", i=4),
+        )
+        att_codes = keep.tile([P, M], U32, name="att_codes", align_bytes=64)
+        att_bytes = keep.tile([P, M], U8, name="att_bytes", align_bytes=64)
+        nc.vector.quantize_mx(
+            out=att_codes[:].bitcast(FP8X4), scales=att_bytes[:], in_=att_grouped[:].rearrange("p m t -> p (m t)")
+        )
+
+        def hidden(e0, n):
+            lz = work.tile([P, n, PACK], BF16, name="lz", align_bytes=64)
+            low = work.tile([P, n, PACK], BF16, name="low", align_bytes=64)
+            both = e0 // BANK_EDGES < TWO_READ_BANKS
+            high = work.tile([P, n, PACK], BF16, name="high", align_bytes=64) if both else None
+            for b0 in range(0, n, BANK_EDGES):
+                e = e0 + b0
+                z = zpsum.tile([P, PACK, BANK_EDGES], F32, name="z")
+                c, o = divmod(e, GATHER_EDGES)
+                for t in range(PACK):
+                    for s in range(2):
+                        nc.tensor.matmul_mx(
+                            out=z[:, t, :],
+                            lhsT=w_codes[s][:, t * P : (t + 1) * P].bitcast(FP8X4),
+                            lhsT_scale=w_bytes[s][:, t * P : (t + 1) * P],
+                            rhs=edge_words[s][c][:, o : o + BANK_EDGES].bitcast(FP8X4),
+                            rhs_scale=edge_bytes[s][:, e : e + BANK_EDGES],
+                            start=(s == 0),
+                            stop=(s == 1),
+                        )
+                z_grouped = z[:].rearrange("p t n -> p n t")
+                part = slice(b0, b0 + BANK_EDGES)
+                nc.scalar.activation(out=low[:, part, :], in_=z_grouped, func=ACT.Copy, scale=SLOPE)
+                if both:
+                    nc.scalar.copy(out=high[:, part, :], in_=z_grouped)
+                else:
+                    nc.vector.tensor_tensor(out=lz[:, part, :], in0=z_grouped, in1=low[:, part, :], op=ALU.max)
+            if both:
+                nc.vector.tensor_tensor(out=lz[:], in0=high[:], in1=low[:], op=ALU.max)
+            return lz
+
+        def score(lz, n):
+            codes = work.tile([P, n], U32, name="lz_codes", align_bytes=64)
+            scales = work.tile([P, n], U8, name="lz_bytes", align_bytes=64)
+            nc.vector.quantize_mx(out=codes[:].bitcast(FP8X4), scales=scales[:], in_=lz[:].rearrange("p n t -> p (n t)"))
+            b = bpsum.tile([M, n], F32, name="b")
+            nc.tensor.matmul_mx(
+                out=b[:],
+                lhsT=att_codes[:].bitcast(FP8X4),
+                lhsT_scale=att_bytes[:],
+                rhs=codes[:].bitcast(FP8X4),
+                rhs_scale=scales[:],
+                start=True,
+                stop=True,
+            )
+            return b
+
+        def exponentials(b, n):
+            groups = n // DEG
+            b_grouped = b[:].rearrange("m (g e) -> m g e", e=DEG)
+            neg_max = work.tile([M, groups], F32, name="neg_max")
+            nc.vector.tensor_reduce(out=neg_max[:], in_=b_grouped, axis=AXIS_X, op=ALU.max, negate=True)
+            shifted = work.tile([M, groups, DEG], F32, name="shifted")
+            nc.vector.tensor_tensor(
+                out=shifted[:], in0=b_grouped, in1=neg_max[:].unsqueeze(2).to_broadcast([M, groups, DEG]), op=ALU.add
+            )
+            p = work.tile([M, groups, DEG], F32, name="p")
+            nc.scalar.activation(out=p[:], in_=shifted[:], func=ACT.Exp)
+            return p
+
+        def normalise(p, e0, n):
+            groups = n // DEG
+            total = work.tile([M, groups], F32, name="total")
+            nc.vector.tensor_reduce(out=total[:], in_=p[:], axis=AXIS_X, op=ALU.add)
+            inverse = work.tile([M, groups], F32, name="inverse")
+            nc.vector.reciprocal(out=inverse[:], in_=total[:])
+            y = work.tile([M, groups, DEG], F32, name="y")
+            nc.vector.scalar_tensor_tensor(
+                out=y[:],
+                in0=p[:],
+                scalar=float(DEG),
+                in1=inverse[:].unsqueeze(2).to_broadcast([M, groups, DEG]),
+                op0=ALU.mult,
+                op1=ALU.mult,
+            )
+            nc.sync.dma_start(out[:, e0 : e0 + n], y[:].rearrange("m g e -> m (g e)"))
+
+        starts = [sum(CHUNKS[:c]) for c in range(len(CHUNKS))]
+        lzs, bs, ps = {}, {}, {}
+        for step in range(len(CHUNKS) + 3):
+            if step < len(CHUNKS):
+                lzs[step] = hidden(starts[step], CHUNKS[step])
+            if 0 <= step - 1 < len(CHUNKS):
+                bs[step - 1] = score(lzs[step - 1], CHUNKS[step - 1])
+            if 0 <= step - 2 < len(CHUNKS):
+                ps[step - 2] = exponentials(bs[step - 2], CHUNKS[step - 2])
+            if 0 <= step - 3 < len(CHUNKS):
+                normalise(ps[step - 3], starts[step - 3], CHUNKS[step - 3])

@@ -23,8 +23,7 @@ SLOPE = 0.2
 BANK_EDGES = 128
 GATHER_EDGES = 256
 HALVES = 2
-CHUNKS = [256,256,256,256]
-TWO_READ_BANKS = 8
+ONE_READ_BANKS = ()
 
 
 def tile_attend_gatv2_kernel(tc, x_words, x_scales, wl, wr, att, offs, offs2, out):
@@ -32,8 +31,9 @@ def tile_attend_gatv2_kernel(tc, x_words, x_scales, wl, wr, att, offs, offs2, ou
     with ExitStack() as ctx:
         keep = ctx.enter_context(tc.tile_pool(name="keep", bufs=1))
         work = ctx.enter_context(tc.tile_pool(name="work", bufs=4))
-        zpsum = ctx.enter_context(tc.psum_pool(name="zpsum", bufs=6))
-        bpsum = ctx.enter_context(tc.psum_pool(name="bpsum", bufs=2))
+        late = ctx.enter_context(tc.tile_pool(name="late", bufs=1))
+        zpsum = ctx.enter_context(tc.psum_pool(name="zpsum", bufs=2))
+        bpsum = ctx.enter_context(tc.psum_pool(name="bpsum", bufs=4))
 
         lists = []
         for name, src in (("src_list", offs), ("dst_list", offs2)):
@@ -87,6 +87,18 @@ def tile_attend_gatv2_kernel(tc, x_words, x_scales, wl, wr, att, offs, offs2, ou
             nc.vector.quantize_mx(
                 out=codes[:].bitcast(FP8X4), scales=scales[:], in_=grouped[:].rearrange("p t c u r j -> p (t c u r j)")
             )
+            if s == 0:
+                for rep in range(4):
+                    heat = bpsum.tile([M, F], F32, name="b")
+                    nc.tensor.matmul_mx(
+                        out=heat[:],
+                        lhsT=codes[:, 0:P].bitcast(FP8X4),
+                        lhsT_scale=scales[:, 0:P],
+                        rhs=codes[:].bitcast(FP8X4),
+                        rhs_scale=scales[:],
+                        start=True,
+                        stop=True,
+                    )
             w_codes.append(codes)
             w_bytes.append(scales)
 
@@ -111,9 +123,11 @@ def tile_attend_gatv2_kernel(tc, x_words, x_scales, wl, wr, att, offs, offs2, ou
 
         def hidden(e0, n):
             lz = work.tile([P, n, PACK], BF16, name="lz", align_bytes=64)
-            low = work.tile([P, n, PACK], BF16, name="low", align_bytes=64)
-            both = e0 // BANK_EDGES < TWO_READ_BANKS
-            high = work.tile([P, n, PACK], BF16, name="high", align_bytes=64) if both else None
+            twice = [b0 for b0 in range(0, n, BANK_EDGES) if (e0 + b0) // BANK_EDGES not in ONE_READ_BANKS]
+            wide = len(twice) * BANK_EDGES
+            if wide:
+                low = work.tile([P, wide, PACK], BF16, name="low", align_bytes=64)
+                high = work.tile([P, wide, PACK], BF16, name="high", align_bytes=64)
             for b0 in range(0, n, BANK_EDGES):
                 e = e0 + b0
                 z = zpsum.tile([P, PACK, BANK_EDGES], F32, name="z")
@@ -131,22 +145,23 @@ def tile_attend_gatv2_kernel(tc, x_words, x_scales, wl, wr, att, offs, offs2, ou
                         )
                 z_grouped = z[:].rearrange("p t n -> p n t")
                 part = slice(b0, b0 + BANK_EDGES)
-                nc.scalar.activation(out=low[:, part, :], in_=z_grouped, func=ACT.Copy, scale=SLOPE)
-                if both:
+                if b0 in twice:
+                    nc.scalar.activation(out=low[:, part, :], in_=z_grouped, func=ACT.Copy, scale=SLOPE)
                     nc.scalar.copy(out=high[:, part, :], in_=z_grouped)
+                    if b0 == twice[-1]:
+                        nc.vector.tensor_tensor(out=lz[:, 0:wide, :], in0=high[:], in1=low[:], op=ALU.max)
                 else:
-                    nc.vector.tensor_tensor(out=lz[:, part, :], in0=z_grouped, in1=low[:, part, :], op=ALU.max)
-            if both:
-                nc.vector.tensor_tensor(out=lz[:], in0=high[:], in1=low[:], op=ALU.max)
+                    single = late.tile([P, BANK_EDGES, PACK], BF16, name="single%d" % e, align_bytes=64)
+                    nc.scalar.activation(out=single[:], in_=z_grouped, func=ACT.Copy, scale=SLOPE)
+                    nc.vector.tensor_tensor(out=lz[:, part, :], in0=z_grouped, in1=single[:], op=ALU.max)
             return lz
 
-        def score(lz, n):
+        def score(lz, n, b, o):
             codes = work.tile([P, n], U32, name="lz_codes", align_bytes=64)
             scales = work.tile([P, n], U8, name="lz_bytes", align_bytes=64)
             nc.vector.quantize_mx(out=codes[:].bitcast(FP8X4), scales=scales[:], in_=lz[:].rearrange("p n t -> p (n t)"))
-            b = bpsum.tile([M, n], F32, name="b")
             nc.tensor.matmul_mx(
-                out=b[:],
+                out=b[:, o : o + n],
                 lhsT=att_codes[:].bitcast(FP8X4),
                 lhsT_scale=att_bytes[:],
                 rhs=codes[:].bitcast(FP8X4),
@@ -154,46 +169,73 @@ def tile_attend_gatv2_kernel(tc, x_words, x_scales, wl, wr, att, offs, offs2, ou
                 start=True,
                 stop=True,
             )
-            return b
 
-        def exponentials(b, n):
-            groups = n // DEG
+        neg_max = keep.tile([M, G], F32, name="neg_max")
+        shifted = keep.tile([M, G, DEG], F32, name="shifted")
+        ps = {}
+        total = keep.tile([M, G], F32, name="total")
+        inverse = keep.tile([M, G], F32, name="inverse")
+        y = keep.tile([M, G, DEG], F32, name="y")
+
+        def shift(b, e0, n):
+            gs = slice(e0 // DEG, (e0 + n) // DEG)
             b_grouped = b[:].rearrange("m (g e) -> m g e", e=DEG)
-            neg_max = work.tile([M, groups], F32, name="neg_max")
-            nc.vector.tensor_reduce(out=neg_max[:], in_=b_grouped, axis=AXIS_X, op=ALU.max, negate=True)
-            shifted = work.tile([M, groups, DEG], F32, name="shifted")
+            nc.vector.tensor_reduce(out=neg_max[:, gs], in_=b_grouped, axis=AXIS_X, op=ALU.max, negate=True)
             nc.vector.tensor_tensor(
-                out=shifted[:], in0=b_grouped, in1=neg_max[:].unsqueeze(2).to_broadcast([M, groups, DEG]), op=ALU.add
+                out=shifted[:, gs, :], in0=b_grouped, in1=neg_max[:, gs].unsqueeze(2).to_broadcast([M, n // DEG, DEG]), op=ALU.add
             )
-            p = work.tile([M, groups, DEG], F32, name="p")
-            nc.scalar.activation(out=p[:], in_=shifted[:], func=ACT.Exp)
-            return p
 
-        def normalise(p, e0, n):
-            groups = n // DEG
-            total = work.tile([M, groups], F32, name="total")
-            nc.vector.tensor_reduce(out=total[:], in_=p[:], axis=AXIS_X, op=ALU.add)
-            inverse = work.tile([M, groups], F32, name="inverse")
-            nc.vector.reciprocal(out=inverse[:], in_=total[:])
-            y = work.tile([M, groups, DEG], F32, name="y")
+        def exponentials(e0, n):
+            gs = slice(e0 // DEG, (e0 + n) // DEG)
+            ps[e0] = late.tile([M, n // DEG, DEG], F32, name="p%d" % e0)
+            nc.scalar.activation(out=ps[e0][:], in_=shifted[:, gs, :], func=ACT.Exp)
+
+        def sums(e0, n):
+            gs = slice(e0 // DEG, (e0 + n) // DEG)
+            nc.vector.tensor_reduce(out=total[:, gs], in_=ps[e0][:], axis=AXIS_X, op=ALU.add)
+
+        def normalise_aside(e0, n):
+            gs = slice(e0 // DEG, (e0 + n) // DEG)
+            plain = keep.tile([M, n // DEG], F32, name="plain%d" % e0)
+            scaled = keep.tile([M, n // DEG], F32, name="scaled%d" % e0)
+            y_aside = keep.tile([M, n // DEG, DEG], F32, name="y_aside%d" % e0)
+            nc.vector.reciprocal(out=plain[:], in_=total[:, gs])
+            nc.gpsimd.tensor_scalar(out=scaled[:], in0=plain[:], scalar1=float(DEG), scalar2=0.0, op0=ALU.mult, op1=ALU.add)
+            nc.gpsimd.tensor_tensor(
+                out=y_aside[:], in0=ps[e0][:], in1=scaled[:].unsqueeze(2).to_broadcast([M, n // DEG, DEG]), op=ALU.mult
+            )
+            nc.sync.dma_start(out[:, e0 : e0 + n], y_aside[:].rearrange("m g e -> m (g e)"))
+
+        def normalise(e0, n):
+            gs = slice(e0 // DEG, (e0 + n) // DEG)
+            nc.vector.reciprocal(out=inverse[:, gs], in_=total[:, gs])
             nc.vector.scalar_tensor_tensor(
-                out=y[:],
-                in0=p[:],
+                out=y[:, gs, :],
+                in0=ps[e0][:],
                 scalar=float(DEG),
-                in1=inverse[:].unsqueeze(2).to_broadcast([M, groups, DEG]),
+                in1=inverse[:, gs].unsqueeze(2).to_broadcast([M, n // DEG, DEG]),
                 op0=ALU.mult,
                 op1=ALU.mult,
             )
-            nc.sync.dma_start(out[:, e0 : e0 + n], y[:].rearrange("m g e -> m (g e)"))
+            nc.sync.dma_start(out[:, e0 : e0 + n], y[:, gs, :].rearrange("m g e -> m (g e)"))
 
-        starts = [sum(CHUNKS[:c]) for c in range(len(CHUNKS))]
-        lzs, bs, ps = {}, {}, {}
-        for step in range(len(CHUNKS) + 3):
-            if step < len(CHUNKS):
-                lzs[step] = hidden(starts[step], CHUNKS[step])
-            if 0 <= step - 1 < len(CHUNKS):
-                bs[step - 1] = score(lzs[step - 1], CHUNKS[step - 1])
-            if 0 <= step - 2 < len(CHUNKS):
-                ps[step - 2] = exponentials(bs[step - 2], CHUNKS[step - 2])
-            if 0 <= step - 3 < len(CHUNKS):
-                normalise(ps[step - 3], starts[step - 3], CHUNKS[step - 3])
+        b0 = bpsum.tile([M, 512], F32, name="b")
+        score(hidden(0, 256), 256, b0, 0)
+        score(hidden(256, 256), 256, b0, 256)
+        shift(b0, 0, 512)
+        b1 = bpsum.tile([M, 384], F32, name="b")
+        score(hidden(512, 256), 256, b1, 0)
+        score(hidden(768, 128), 128, b1, 256)
+        b2 = bpsum.tile([M, 128], F32, name="b")
+        score(hidden(896, 128), 128, b2, 0)
+        exponentials(0, 512)
+        sums(0, 512)
+        normalise_aside(0, 512)
+        shift(b1, 512, 384)
+        exponentials(512, 384)
+        shift(b2, 896, 128)
+        exponentials(896, 128)
+        sums(512, 384)
+        normalise(512, 384)
+        sums(896, 128)
+        normalise(896, 128)

@@ -3,7 +3,7 @@ from contextlib import ExitStack
 import concourse.mybir as mybir
 
 K, T, I, F, M, G = 512, 2048, 1024, 512, 128, 64
-FLOPS = 2 * K * F * I * 2 + 2 * F * M * I
+FLOPS = 2 * (2 * K * F * I) + 2 * F * M * I
 
 F32 = mybir.dt.float32
 BF16 = mybir.dt.bfloat16
@@ -18,224 +18,220 @@ AXIS_X = mybir.AxisListType.X
 
 P = 128
 PACK = 4
+RUN = 4
 DEG = I // G
 SLOPE = 0.2
 BANK_EDGES = 128
-GATHER_EDGES = 256
-HALVES = 2
-ONE_READ_BANKS = ()
+WEIGHT_LOADS = ((128, 384), (256, 256))
+GATHERS = (256, 256, 512)
+WIDE, NARROW = 256, 128
+WIDE_TILES = 3
+WARM_PASSES = 4
 
 
 def tile_attend_gatv2_kernel(tc, x_words, x_scales, wl, wr, att, offs, offs2, out):
     nc = tc.nc
     with ExitStack() as ctx:
         keep = ctx.enter_context(tc.tile_pool(name="keep", bufs=1))
-        work = ctx.enter_context(tc.tile_pool(name="work", bufs=4))
-        late = ctx.enter_context(tc.tile_pool(name="late", bufs=1))
-        zpsum = ctx.enter_context(tc.psum_pool(name="zpsum", bufs=2))
-        bpsum = ctx.enter_context(tc.psum_pool(name="bpsum", bufs=4))
+        z_psum = ctx.enter_context(tc.psum_pool(name="z_psum", bufs=2))
+        b_psum = ctx.enter_context(tc.psum_pool(name="b_psum", bufs=4))
+
+        def quantise(grouped, name):
+            columns = grouped.shape[1] // PACK
+            words = keep.tile([P, columns], U32, name=name + "_words", align_bytes=64)
+            scales = keep.tile([P, columns], U8, name=name + "_scales", align_bytes=64)
+            nc.vector.quantize_mx(out=words[:].bitcast(FP8X4), scales=scales[:], in_=grouped)
+            return words, scales
+
+        def product(result, left, right, start, stop):
+            nc.tensor.matmul_mx(
+                out=result,
+                lhsT=left[0].bitcast(FP8X4),
+                lhsT_scale=left[1],
+                rhs=right[0].bitcast(FP8X4),
+                rhs_scale=right[1],
+                start=start,
+                stop=stop,
+            )
 
         lists = []
-        for name, src in (("src_list", offs), ("dst_list", offs2)):
-            tile = keep.tile([P, I // 16], U16, name=name)
-            nc.sync.dma_start(tile[:], src)
-            lists.append(tile)
+        for side, source in enumerate((offs, offs2)):
+            lists.append(keep.tile([P, I // 16], U16, name="list%d" % side))
+            nc.sync.dma_start(lists[side][:], source)
 
-        x_bytes = keep.tile([P, T], U8, name="x_bytes", align_bytes=64)
-        nc.vector.memset(x_bytes[:].bitcast(I32), 0)
-        for q in range(4):
-            nc.sync.dma_start(x_bytes[32 * q : 32 * q + 4, :].bitcast(I32), x_scales[0, 4 * q : 4 * q + 4, :].bitcast(I32))
+        w_rows = [w.rearrange("(p j) f -> p j f", j=PACK) for w in (wl, wr)]
+        w_pieces = [
+            (side, sum(widths[:c]), width) for side, widths in enumerate(WEIGHT_LOADS) for c, width in enumerate(widths)
+        ]
+        w_raw = {}
 
-        warm = keep.tile([P, 1], F32, name="warm")
-        warm_out = keep.tile([P, 1], F32, name="warm_out")
-        nc.gpsimd.memset(warm[:], 0.0)
-        nc.scalar.activation(out=warm_out[:], in_=warm[:], func=ACT.Exp)
+        def load_weights(side, f0, width):
+            w_raw[side, f0] = keep.tile([P, PACK, width], F32, name="w_raw%d_%d" % (side, f0))
+            nc.sync.dma_start(w_raw[side, f0][:], w_rows[side][:, :, f0 : f0 + width])
 
-        half = F // HALVES
-        w_raw = []
-        for name, w in (("wl", wl), ("wr", wr)):
-            rows = w.rearrange("(p j) f -> p j f", j=PACK)
-            for c in range(HALVES):
-                raw = keep.tile([P, PACK, half], F32, name="%s_raw%d" % (name, c))
-                nc.sync.dma_start(raw[:], rows[:, :, c * half : (c + 1) * half])
-                w_raw.append(raw)
+        load_weights(*w_pieces[0])
 
-        x_tile = keep.tile([P, T], U32, name="x_tile", align_bytes=64)
-        nc.sync.dma_start(x_tile[:].bitcast(I32), x_words[0].rearrange("p n t -> p (n t)").bitcast(I32))
-
-        att_raw = keep.tile([P, PACK, M], F32, name="att_raw")
-        att_rows = att.rearrange("(u t r) m -> r u t m", t=PACK, r=4)
-        for r in range(4):
-            nc.sync.dma_start(att_raw[r:P:4, :, :], att_rows[r])
-
-        edge_bytes = []
-        for s in range(2):
-            picked = keep.tile([P, I], U8, name="edge_bytes%d" % s, align_bytes=64)
-            nc.vector.tensor_copy(out=picked[:], in_=x_bytes[:].indirect(lists[s][:]))
-            edge_bytes.append(picked)
-
-        w_codes, w_bytes = [], []
-        for s in range(2):
-            grouped = keep.tile([P, PACK, HALVES, half // 16, 4, PACK], BF16, name="w_grouped%d" % s, align_bytes=64)
-            for c in range(HALVES):
-                nc.scalar.copy(
-                    out=grouped[:, :, c, :, :, :].rearrange("p t u r j -> p t u j r"),
-                    in_=w_raw[HALVES * s + c][:].rearrange("p j (u t r) -> p t u j r", t=PACK, r=4),
-                )
-            codes = keep.tile([P, F], U32, name="w_codes%d" % s, align_bytes=64)
-            scales = keep.tile([P, F], U8, name="w_bytes%d" % s, align_bytes=64)
-            nc.vector.quantize_mx(
-                out=codes[:].bitcast(FP8X4), scales=scales[:], in_=grouped[:].rearrange("p t c u r j -> p (t c u r j)")
+        node_scales = keep.tile([P, T], U8, name="node_scales", align_bytes=64)
+        nc.vector.memset(node_scales[:].bitcast(I32), 0)
+        for quadrant in range(4):
+            nc.sync.dma_start(
+                node_scales[32 * quadrant : 32 * quadrant + 4, :].bitcast(I32),
+                x_scales[0, 4 * quadrant : 4 * quadrant + 4, :].bitcast(I32),
             )
-            if s == 0:
-                for rep in range(4):
-                    heat = bpsum.tile([M, F], F32, name="b")
-                    nc.tensor.matmul_mx(
-                        out=heat[:],
-                        lhsT=codes[:, 0:P].bitcast(FP8X4),
-                        lhsT_scale=scales[:, 0:P],
-                        rhs=codes[:].bitcast(FP8X4),
-                        rhs_scale=scales[:],
-                        start=True,
-                        stop=True,
-                    )
-            w_codes.append(codes)
-            w_bytes.append(scales)
 
-        edge_words = [[], []]
-        for c in range(I // GATHER_EDGES):
-            cols = slice(c * GATHER_EDGES // 16, (c + 1) * GATHER_EDGES // 16)
-            for s in range(2):
-                picked = keep.tile([P, GATHER_EDGES], U32, name="edge_words%d_%d" % (s, c), align_bytes=64)
-                nc.vector.tensor_copy(out=picked[:], in_=x_tile[:].indirect(lists[s][:, cols]))
-                edge_words[s].append(picked)
+        warm_in = keep.tile([P, 1], F32, name="warm_in")
+        warm_out = keep.tile([P, 1], F32, name="warm_out")
+        nc.gpsimd.memset(warm_in[:], 0.0)
+        nc.scalar.activation(out=warm_out[:], in_=warm_in[:], func=ACT.Exp)
+
+        for piece in w_pieces[1:]:
+            load_weights(*piece)
+
+        node_words = keep.tile([P, T], U32, name="node_words", align_bytes=64)
+        nc.sync.dma_start(node_words[:].bitcast(I32), x_words[0].rearrange("p n j -> p (n j)").bitcast(I32))
+
+        att_raw = keep.tile([P, PACK, M], F32, name="att_raw", align_bytes=64)
+        att_rows = att.rearrange("(u t r) m -> r u t m", t=PACK, r=RUN)
+        for r in range(RUN):
+            nc.sync.dma_start(att_raw[r:P:RUN, :, :], att_rows[r])
+
+        edge_scales = []
+        for side in range(2):
+            edge_scales.append(keep.tile([P, I], U8, name="edge_scales%d" % side, align_bytes=64))
+            nc.vector.tensor_copy(out=edge_scales[side][:], in_=node_scales[:].indirect(lists[side][:]))
+
+        weights = []
+        for side in range(2):
+            w_grouped = keep.tile([P, PACK, F // 16, RUN, PACK], BF16, name="w_grouped%d" % side, align_bytes=64)
+            for owner, f0, width in w_pieces:
+                if owner == side:
+                    nc.scalar.copy(
+                        out=w_grouped[:, :, f0 // 16 : (f0 + width) // 16, :, :].rearrange("p t u r j -> p t u j r"),
+                        in_=w_raw[side, f0][:].rearrange("p j (u t r) -> p t u j r", t=PACK, r=RUN),
+                    )
+            weights.append(quantise(w_grouped[:].rearrange("p t u r j -> p (t u r j)"), "w%d" % side))
+            if side == 0:
+                words, scales = weights[side]
+                for repeat in range(WARM_PASSES):
+                    unread = b_psum.tile([M, F], F32, name="b")
+                    product(unread[:], (words[:, 0:P], scales[:, 0:P]), (words[:], scales[:]), True, True)
+
+        edge_words = {}
+        for c, count in enumerate(GATHERS):
+            first = sum(GATHERS[:c])
+            for side in range(2):
+                picked = keep.tile([P, count], U32, name="edge_words%d_%d" % (side, first), align_bytes=64)
+                offsets = lists[side][:, first // 16 : (first + count) // 16]
+                nc.vector.tensor_copy(out=picked[:], in_=node_words[:].indirect(offsets))
+                for o in range(0, count, BANK_EDGES):
+                    edge_words[side, first + o] = picked[:, o : o + BANK_EDGES]
 
         att_grouped = keep.tile([P, M, PACK], BF16, name="att_grouped", align_bytes=64)
         nc.scalar.copy(
-            out=att_grouped[:].rearrange("p (c i) t -> p c t i", i=4),
-            in_=att_raw[:].rearrange("p t (c i) -> p c t i", i=4),
+            out=att_grouped[:].rearrange("p (c r) t -> p c t r", r=RUN),
+            in_=att_raw[:].rearrange("p t (c r) -> p c t r", r=RUN),
         )
-        att_codes = keep.tile([P, M], U32, name="att_codes", align_bytes=64)
-        att_bytes = keep.tile([P, M], U8, name="att_bytes", align_bytes=64)
-        nc.vector.quantize_mx(
-            out=att_codes[:].bitcast(FP8X4), scales=att_bytes[:], in_=att_grouped[:].rearrange("p m t -> p (m t)")
-        )
+        att_words, att_scales = quantise(att_grouped[:].rearrange("p m t -> p (m t)"), "att")
 
-        def hidden(e0, n):
-            lz = work.tile([P, n, PACK], BF16, name="lz", align_bytes=64)
-            twice = [b0 for b0 in range(0, n, BANK_EDGES) if (e0 + b0) // BANK_EDGES not in ONE_READ_BANKS]
-            wide = len(twice) * BANK_EDGES
-            if wide:
-                low = work.tile([P, wide, PACK], BF16, name="low", align_bytes=64)
-                high = work.tile([P, wide, PACK], BF16, name="high", align_bytes=64)
-            for b0 in range(0, n, BANK_EDGES):
-                e = e0 + b0
-                z = zpsum.tile([P, PACK, BANK_EDGES], F32, name="z")
-                c, o = divmod(e, GATHER_EDGES)
+        def scores(e0, n):
+            low_tag = "att_raw" if e0 == 0 else "low%d" % e0
+            low = keep.tile([P, n, PACK], BF16, name="low%d" % e0, tag=low_tag, align_bytes=64)
+            high = keep.tile([P, n, PACK], BF16, name="high%d" % e0, align_bytes=64)
+            for o in range(0, n, BANK_EDGES):
+                e = e0 + o
+                z = z_psum.tile([P, PACK, BANK_EDGES], F32, name="z")
                 for t in range(PACK):
-                    for s in range(2):
-                        nc.tensor.matmul_mx(
-                            out=z[:, t, :],
-                            lhsT=w_codes[s][:, t * P : (t + 1) * P].bitcast(FP8X4),
-                            lhsT_scale=w_bytes[s][:, t * P : (t + 1) * P],
-                            rhs=edge_words[s][c][:, o : o + BANK_EDGES].bitcast(FP8X4),
-                            rhs_scale=edge_bytes[s][:, e : e + BANK_EDGES],
-                            start=(s == 0),
-                            stop=(s == 1),
+                    columns = slice(t * P, (t + 1) * P)
+                    for side in range(2):
+                        product(
+                            z[:, t, :],
+                            (weights[side][0][:, columns], weights[side][1][:, columns]),
+                            (edge_words[side, e], edge_scales[side][:, e : e + BANK_EDGES]),
+                            side == 0,
+                            side == 1,
                         )
                 z_grouped = z[:].rearrange("p t n -> p n t")
-                part = slice(b0, b0 + BANK_EDGES)
-                if b0 in twice:
-                    nc.scalar.activation(out=low[:, part, :], in_=z_grouped, func=ACT.Copy, scale=SLOPE)
-                    nc.scalar.copy(out=high[:, part, :], in_=z_grouped)
-                    if b0 == twice[-1]:
-                        nc.vector.tensor_tensor(out=lz[:, 0:wide, :], in0=high[:], in1=low[:], op=ALU.max)
-                else:
-                    single = late.tile([P, BANK_EDGES, PACK], BF16, name="single%d" % e, align_bytes=64)
-                    nc.scalar.activation(out=single[:], in_=z_grouped, func=ACT.Copy, scale=SLOPE)
-                    nc.vector.tensor_tensor(out=lz[:, part, :], in0=z_grouped, in1=single[:], op=ALU.max)
-            return lz
+                nc.scalar.activation(out=low[:, o : o + BANK_EDGES, :], in_=z_grouped, func=ACT.Copy, scale=SLOPE)
+                nc.scalar.copy(out=high[:, o : o + BANK_EDGES, :], in_=z_grouped)
+            lz = keep.tile([P, n, PACK], BF16, name="lz%d" % e0, align_bytes=64)
+            nc.vector.tensor_tensor(out=lz[:], in0=high[:], in1=low[:], op=ALU.max)
+            lz_words, lz_scales = quantise(lz[:].rearrange("p n t -> p (n t)"), "lz%d" % e0)
+            b = b_psum.tile([M, n], F32, name="b")
+            product(b[:], (att_words[:], att_scales[:]), (lz_words[:], lz_scales[:]), True, True)
+            return b[:].rearrange("m (g e) -> m g e", e=DEG)
 
-        def score(lz, n, b, o):
-            codes = work.tile([P, n], U32, name="lz_codes", align_bytes=64)
-            scales = work.tile([P, n], U8, name="lz_bytes", align_bytes=64)
-            nc.vector.quantize_mx(out=codes[:].bitcast(FP8X4), scales=scales[:], in_=lz[:].rearrange("p n t -> p (n t)"))
-            nc.tensor.matmul_mx(
-                out=b[:, o : o + n],
-                lhsT=att_codes[:].bitcast(FP8X4),
-                lhsT_scale=att_bytes[:],
-                rhs=codes[:].bitcast(FP8X4),
-                rhs_scale=scales[:],
-                start=True,
-                stop=True,
-            )
+        shifted = keep.tile([M, WIDE_TILES * WIDE // DEG, DEG], F32, name="shifted")
+        terms = keep.tile([M, G, DEG], F32, name="terms")
+        totals = keep.tile([M, G], F32, name="totals")
+        inverses = keep.tile([M, G], F32, name="inverses")
+        result = keep.tile([M, G, DEG], F32, name="result")
 
-        neg_max = keep.tile([M, G], F32, name="neg_max")
-        shifted = keep.tile([M, G, DEG], F32, name="shifted")
-        ps = {}
-        total = keep.tile([M, G], F32, name="total")
-        inverse = keep.tile([M, G], F32, name="inverse")
-        y = keep.tile([M, G, DEG], F32, name="y")
+        def targets(e0, n):
+            return slice(e0 // DEG, (e0 + n) // DEG)
+
+        def negated_maxima(b, e0, n):
+            max_tag = "lz%d" % WIDE if e0 == 0 else "neg_max%d" % e0
+            neg_max = keep.tile([M, n // DEG], F32, name="neg_max%d" % e0, tag=max_tag, align_bytes=64)
+            nc.vector.tensor_reduce(out=neg_max[:], in_=b, axis=AXIS_X, op=ALU.max, negate=True)
+            return neg_max
 
         def shift(b, e0, n):
-            gs = slice(e0 // DEG, (e0 + n) // DEG)
-            b_grouped = b[:].rearrange("m (g e) -> m g e", e=DEG)
-            nc.vector.tensor_reduce(out=neg_max[:, gs], in_=b_grouped, axis=AXIS_X, op=ALU.max, negate=True)
-            nc.vector.tensor_tensor(
-                out=shifted[:, gs, :], in0=b_grouped, in1=neg_max[:, gs].unsqueeze(2).to_broadcast([M, n // DEG, DEG]), op=ALU.add
-            )
+            neg_max = negated_maxima(b, e0, n)
+            spread = neg_max[:].unsqueeze(2).to_broadcast([M, n // DEG, DEG])
+            nc.vector.tensor_tensor(out=shifted[:, targets(e0, n), :], in0=b, in1=spread, op=ALU.add)
 
         def exponentials(e0, n):
-            gs = slice(e0 // DEG, (e0 + n) // DEG)
-            ps[e0] = late.tile([M, n // DEG, DEG], F32, name="p%d" % e0)
-            nc.scalar.activation(out=ps[e0][:], in_=shifted[:, gs, :], func=ACT.Exp)
+            nc.scalar.activation(out=terms[:, targets(e0, n), :], in_=shifted[:, targets(e0, n), :], func=ACT.Exp)
 
         def sums(e0, n):
-            gs = slice(e0 // DEG, (e0 + n) // DEG)
-            nc.vector.tensor_reduce(out=total[:, gs], in_=ps[e0][:], axis=AXIS_X, op=ALU.add)
+            nc.vector.tensor_reduce(out=totals[:, targets(e0, n)], in_=terms[:, targets(e0, n), :], axis=AXIS_X, op=ALU.add)
 
-        def normalise_aside(e0, n):
-            gs = slice(e0 // DEG, (e0 + n) // DEG)
-            plain = keep.tile([M, n // DEG], F32, name="plain%d" % e0)
-            scaled = keep.tile([M, n // DEG], F32, name="scaled%d" % e0)
-            y_aside = keep.tile([M, n // DEG, DEG], F32, name="y_aside%d" % e0)
-            nc.vector.reciprocal(out=plain[:], in_=total[:, gs])
-            nc.gpsimd.tensor_scalar(out=scaled[:], in0=plain[:], scalar1=float(DEG), scalar2=0.0, op0=ALU.mult, op1=ALU.add)
-            nc.gpsimd.tensor_tensor(
-                out=y_aside[:], in0=ps[e0][:], in1=scaled[:].unsqueeze(2).to_broadcast([M, n // DEG, DEG]), op=ALU.mult
-            )
-            nc.sync.dma_start(out[:, e0 : e0 + n], y_aside[:].rearrange("m g e -> m (g e)"))
+        def exponentials_and_sums(b, e0, n):
+            neg_max = negated_maxima(b, e0, n)
+            for g in range(n // DEG):
+                target = e0 // DEG + g
+                nc.scalar.activation(
+                    out=terms[:, target, :],
+                    in_=b[:, g, :],
+                    func=ACT.Exp,
+                    bias=neg_max[:, g : g + 1],
+                    accum_out=totals[:, target : target + 1],
+                )
 
-        def normalise(e0, n):
-            gs = slice(e0 // DEG, (e0 + n) // DEG)
-            nc.vector.reciprocal(out=inverse[:, gs], in_=total[:, gs])
+        def invert(e0, n):
+            nc.vector.reciprocal(out=inverses[:, targets(e0, n)], in_=totals[:, targets(e0, n)])
+
+        def normalise_and_store(e0, n):
             nc.vector.scalar_tensor_tensor(
-                out=y[:, gs, :],
-                in0=ps[e0][:],
+                out=result[:, targets(e0, n), :],
+                in0=terms[:, targets(e0, n), :],
                 scalar=float(DEG),
-                in1=inverse[:, gs].unsqueeze(2).to_broadcast([M, n // DEG, DEG]),
+                in1=inverses[:, targets(e0, n)].unsqueeze(2).to_broadcast([M, n // DEG, DEG]),
                 op0=ALU.mult,
                 op1=ALU.mult,
             )
-            nc.sync.dma_start(out[:, e0 : e0 + n], y[:, gs, :].rearrange("m g e -> m (g e)"))
+            nc.sync.dma_start(out[:, e0 : e0 + n], result[:, targets(e0, n), :].rearrange("m g e -> m (g e)"))
 
-        b0 = bpsum.tile([M, 512], F32, name="b")
-        score(hidden(0, 256), 256, b0, 0)
-        score(hidden(256, 256), 256, b0, 256)
-        shift(b0, 0, 512)
-        b1 = bpsum.tile([M, 384], F32, name="b")
-        score(hidden(512, 256), 256, b1, 0)
-        score(hidden(768, 128), 128, b1, 256)
-        b2 = bpsum.tile([M, 128], F32, name="b")
-        score(hidden(896, 128), 128, b2, 0)
-        exponentials(0, 512)
-        sums(0, 512)
-        normalise_aside(0, 512)
-        shift(b1, 512, 384)
-        exponentials(512, 384)
-        shift(b2, 896, 128)
-        exponentials(896, 128)
-        sums(512, 384)
-        normalise(512, 384)
-        sums(896, 128)
-        normalise(896, 128)
+        third = 2 * WIDE
+        fourth = third + WIDE
+        last = fourth + NARROW
+        b_first = scores(0, WIDE)
+        b_second = scores(WIDE, WIDE)
+        shift(b_first, 0, WIDE)
+        shift(b_second, WIDE, WIDE)
+        b_third = scores(third, WIDE)
+        b_fourth = scores(fourth, NARROW)
+        b_last = scores(last, NARROW)
+        exponentials(0, third)
+        shift(b_third, third, WIDE)
+        exponentials(third, WIDE)
+        exponentials_and_sums(b_fourth, fourth, NARROW)
+        exponentials_and_sums(b_last, last, NARROW)
+        sums(0, third)
+        sums(third, WIDE)
+        invert(0, third)
+        invert(third, last - third)
+        normalise_and_store(0, third)
+        invert(last, NARROW)
+        normalise_and_store(third, last - third)
+        normalise_and_store(last, NARROW)

from contextlib import ExitStack

import concourse.mybir as mybir

K, T, I, F, M, G = 512, 2048, 1024, 512, 128, 64
FLOPS = 2 * (2 * K * F * I) + 2 * F * M * I

F32 = mybir.dt.float32
BF16 = mybir.dt.bfloat16
I32 = mybir.dt.int32
U32 = mybir.dt.uint32
U16 = mybir.dt.uint16
U8 = mybir.dt.uint8
FP8X4 = mybir.dt.float8_e4m3fn_x4
ALU = mybir.AluOpType
ACT = mybir.ActivationFunctionType
AXIS_X = mybir.AxisListType.X

P = 128
PACK = 4
RUN = 4
DEG = I // G
SLOPE = 0.2
BANK_EDGES = 128
WEIGHT_LOADS = ((128, 384), (256, 256))
GATHERS = (256, 256, 512)
WIDE, NARROW = 256, 128
WIDE_TILES = 3
WARM_PASSES = 4


def tile_attend_gatv2_kernel(tc, x_words, x_scales, wl, wr, att, offs, offs2, out):
    nc = tc.nc
    with ExitStack() as ctx:
        keep = ctx.enter_context(tc.tile_pool(name="keep", bufs=1))
        z_psum = ctx.enter_context(tc.psum_pool(name="z_psum", bufs=2))
        b_psum = ctx.enter_context(tc.psum_pool(name="b_psum", bufs=4))

        def quantise(grouped, name):
            columns = grouped.shape[1] // PACK
            words = keep.tile([P, columns], U32, name=name + "_words", align_bytes=64)
            scales = keep.tile([P, columns], U8, name=name + "_scales", align_bytes=64)
            nc.vector.quantize_mx(out=words[:].bitcast(FP8X4), scales=scales[:], in_=grouped)
            return words, scales

        def product(result, left, right, start, stop):
            nc.tensor.matmul_mx(
                out=result,
                lhsT=left[0].bitcast(FP8X4),
                lhsT_scale=left[1],
                rhs=right[0].bitcast(FP8X4),
                rhs_scale=right[1],
                start=start,
                stop=stop,
            )

        lists = []
        for side, source in enumerate((offs, offs2)):
            lists.append(keep.tile([P, I // 16], U16, name="list%d" % side))
            nc.sync.dma_start(lists[side][:], source)

        w_rows = [w.rearrange("(p j) f -> p j f", j=PACK) for w in (wl, wr)]
        w_pieces = [
            (side, sum(widths[:c]), width) for side, widths in enumerate(WEIGHT_LOADS) for c, width in enumerate(widths)
        ]
        w_raw = {}

        def load_weights(side, f0, width):
            w_raw[side, f0] = keep.tile([P, PACK, width], F32, name="w_raw%d_%d" % (side, f0))
            nc.sync.dma_start(w_raw[side, f0][:], w_rows[side][:, :, f0 : f0 + width])

        load_weights(*w_pieces[0])

        node_scales = keep.tile([P, T], U8, name="node_scales", align_bytes=64)
        nc.vector.memset(node_scales[:].bitcast(I32), 0)
        for quadrant in range(4):
            nc.sync.dma_start(
                node_scales[32 * quadrant : 32 * quadrant + 4, :].bitcast(I32),
                x_scales[0, 4 * quadrant : 4 * quadrant + 4, :].bitcast(I32),
            )

        warm_in = keep.tile([P, 1], F32, name="warm_in")
        warm_out = keep.tile([P, 1], F32, name="warm_out")
        nc.gpsimd.memset(warm_in[:], 0.0)
        nc.scalar.activation(out=warm_out[:], in_=warm_in[:], func=ACT.Exp)

        for piece in w_pieces[1:]:
            load_weights(*piece)

        node_words = keep.tile([P, T], U32, name="node_words", align_bytes=64)
        nc.sync.dma_start(node_words[:].bitcast(I32), x_words[0].rearrange("p n j -> p (n j)").bitcast(I32))

        att_raw = keep.tile([P, PACK, M], F32, name="att_raw", align_bytes=64)
        att_rows = att.rearrange("(u t r) m -> r u t m", t=PACK, r=RUN)
        for r in range(RUN):
            nc.sync.dma_start(att_raw[r:P:RUN, :, :], att_rows[r])

        edge_scales = []
        for side in range(2):
            edge_scales.append(keep.tile([P, I], U8, name="edge_scales%d" % side, align_bytes=64))
            nc.vector.tensor_copy(out=edge_scales[side][:], in_=node_scales[:].indirect(lists[side][:]))

        weights = []
        for side in range(2):
            w_grouped = keep.tile([P, PACK, F // 16, RUN, PACK], BF16, name="w_grouped%d" % side, align_bytes=64)
            for owner, f0, width in w_pieces:
                if owner == side:
                    nc.scalar.copy(
                        out=w_grouped[:, :, f0 // 16 : (f0 + width) // 16, :, :].rearrange("p t u r j -> p t u j r"),
                        in_=w_raw[side, f0][:].rearrange("p j (u t r) -> p t u j r", t=PACK, r=RUN),
                    )
            weights.append(quantise(w_grouped[:].rearrange("p t u r j -> p (t u r j)"), "w%d" % side))
            if side == 0:
                words, scales = weights[side]
                for repeat in range(WARM_PASSES):
                    unread = b_psum.tile([M, F], F32, name="b")
                    product(unread[:], (words[:, 0:P], scales[:, 0:P]), (words[:], scales[:]), True, True)

        edge_words = {}
        for c, count in enumerate(GATHERS):
            first = sum(GATHERS[:c])
            for side in range(2):
                picked = keep.tile([P, count], U32, name="edge_words%d_%d" % (side, first), align_bytes=64)
                offsets = lists[side][:, first // 16 : (first + count) // 16]
                nc.vector.tensor_copy(out=picked[:], in_=node_words[:].indirect(offsets))
                for o in range(0, count, BANK_EDGES):
                    edge_words[side, first + o] = picked[:, o : o + BANK_EDGES]

        att_grouped = keep.tile([P, M, PACK], BF16, name="att_grouped", align_bytes=64)
        nc.scalar.copy(
            out=att_grouped[:].rearrange("p (c r) t -> p c t r", r=RUN),
            in_=att_raw[:].rearrange("p t (c r) -> p c t r", r=RUN),
        )
        att_words, att_scales = quantise(att_grouped[:].rearrange("p m t -> p (m t)"), "att")

        def scores(e0, n):
            low_tag = "att_raw" if e0 == 0 else "low%d" % e0
            low = keep.tile([P, n, PACK], BF16, name="low%d" % e0, tag=low_tag, align_bytes=64)
            high = keep.tile([P, n, PACK], BF16, name="high%d" % e0, align_bytes=64)
            for o in range(0, n, BANK_EDGES):
                e = e0 + o
                z = z_psum.tile([P, PACK, BANK_EDGES], F32, name="z")
                for t in range(PACK):
                    columns = slice(t * P, (t + 1) * P)
                    for side in range(2):
                        product(
                            z[:, t, :],
                            (weights[side][0][:, columns], weights[side][1][:, columns]),
                            (edge_words[side, e], edge_scales[side][:, e : e + BANK_EDGES]),
                            side == 0,
                            side == 1,
                        )
                z_grouped = z[:].rearrange("p t n -> p n t")
                nc.scalar.activation(out=low[:, o : o + BANK_EDGES, :], in_=z_grouped, func=ACT.Copy, scale=SLOPE)
                nc.scalar.copy(out=high[:, o : o + BANK_EDGES, :], in_=z_grouped)
            lz = keep.tile([P, n, PACK], BF16, name="lz%d" % e0, align_bytes=64)
            nc.vector.tensor_tensor(out=lz[:], in0=high[:], in1=low[:], op=ALU.max)
            lz_words, lz_scales = quantise(lz[:].rearrange("p n t -> p (n t)"), "lz%d" % e0)
            b = b_psum.tile([M, n], F32, name="b")
            product(b[:], (att_words[:], att_scales[:]), (lz_words[:], lz_scales[:]), True, True)
            return b[:].rearrange("m (g e) -> m g e", e=DEG)

        shifted = keep.tile([M, WIDE_TILES * WIDE // DEG, DEG], F32, name="shifted")
        terms = keep.tile([M, G, DEG], F32, name="terms")
        totals = keep.tile([M, G], F32, name="totals")
        inverses = keep.tile([M, G], F32, name="inverses")
        result = keep.tile([M, G, DEG], F32, name="result")

        def targets(e0, n):
            return slice(e0 // DEG, (e0 + n) // DEG)

        def negated_maxima(b, e0, n):
            max_tag = "lz%d" % WIDE if e0 == 0 else "neg_max%d" % e0
            neg_max = keep.tile([M, n // DEG], F32, name="neg_max%d" % e0, tag=max_tag, align_bytes=64)
            nc.vector.tensor_reduce(out=neg_max[:], in_=b, axis=AXIS_X, op=ALU.max, negate=True)
            return neg_max

        def shift(b, e0, n):
            neg_max = negated_maxima(b, e0, n)
            spread = neg_max[:].unsqueeze(2).to_broadcast([M, n // DEG, DEG])
            nc.vector.tensor_tensor(out=shifted[:, targets(e0, n), :], in0=b, in1=spread, op=ALU.add)

        def exponentials(e0, n):
            nc.scalar.activation(out=terms[:, targets(e0, n), :], in_=shifted[:, targets(e0, n), :], func=ACT.Exp)

        def sums(e0, n):
            nc.vector.tensor_reduce(out=totals[:, targets(e0, n)], in_=terms[:, targets(e0, n), :], axis=AXIS_X, op=ALU.add)

        def exponentials_and_sums(b, e0, n):
            neg_max = negated_maxima(b, e0, n)
            for g in range(n // DEG):
                target = e0 // DEG + g
                nc.scalar.activation(
                    out=terms[:, target, :],
                    in_=b[:, g, :],
                    func=ACT.Exp,
                    bias=neg_max[:, g : g + 1],
                    accum_out=totals[:, target : target + 1],
                )

        def invert(e0, n):
            nc.vector.reciprocal(out=inverses[:, targets(e0, n)], in_=totals[:, targets(e0, n)])

        def normalise_and_store(e0, n):
            nc.vector.scalar_tensor_tensor(
                out=result[:, targets(e0, n), :],
                in0=terms[:, targets(e0, n), :],
                scalar=float(DEG),
                in1=inverses[:, targets(e0, n)].unsqueeze(2).to_broadcast([M, n // DEG, DEG]),
                op0=ALU.mult,
                op1=ALU.mult,
            )
            nc.sync.dma_start(out[:, e0 : e0 + n], result[:, targets(e0, n), :].rearrange("m g e -> m (g e)"))

        third = 2 * WIDE
        fourth = third + WIDE
        last = fourth + NARROW
        b_first = scores(0, WIDE)
        b_second = scores(WIDE, WIDE)
        shift(b_first, 0, WIDE)
        shift(b_second, WIDE, WIDE)
        b_third = scores(third, WIDE)
        b_fourth = scores(fourth, NARROW)
        b_last = scores(last, NARROW)
        exponentials(0, third)
        shift(b_third, third, WIDE)
        exponentials(third, WIDE)
        exponentials_and_sums(b_fourth, fourth, NARROW)
        exponentials_and_sums(b_last, last, NARROW)
        sums(0, third)
        sums(third, WIDE)
        invert(0, third)
        invert(third, last - third)
        normalise_and_store(0, third)
        invert(last, NARROW)
        normalise_and_store(third, last - third)
        normalise_and_store(last, NARROW)
